import numpy as np
import ml_dtypes


def mxq(x, axis, fmt="e4m3"):
    dtype, down = {"e4m3": (ml_dtypes.float8_e4m3fn, 7), "e5m2": (ml_dtypes.float8_e5m2, 14)}[fmt]
    v = np.moveaxis(np.asarray(x, np.float32).astype(ml_dtypes.bfloat16).astype(np.float64), axis, -1)
    blocks = v.reshape(v.shape[:-1] + (-1, 32))
    amax = np.abs(blocks).max(-1, keepdims=True)
    byte = np.maximum(np.where(amax > 0, np.frexp(amax)[1] - 1 + 127, 0) - down, 1)
    scale = np.exp2(byte - 127.0)
    codes = (blocks / scale).astype(np.float32).astype(dtype).astype(np.float64)
    return np.moveaxis((codes * scale).reshape(v.shape), -1, axis)


WIDE = False


def mx_kscale(k):
    if not WIDE:
        return np.ones(k)
    levels = np.array([10, -10, 5, -5, 0])
    if k % 512:
        return np.exp2(np.random.permutation(np.resize(levels, k // 32))).repeat(32)
    a = np.empty((k // 512, 16))
    for p in range(k // 512):
        a[p, :8] = np.random.permutation(np.resize(levels, 8))
        for g in range(8):
            far = levels[np.abs(levels - a[p, g]) >= 10]
            a[p, g + 8] = far[np.random.randint(len(far))]
    return np.exp2(a.ravel()).repeat(32)


def f64(x):
    return np.asarray(x).astype(np.float64)


def striped(idx):
    return np.tile(idx.reshape(-1, 16).T, (8, 1)).astype(np.uint16)


def unstriped(offs):
    return offs[:16].T.reshape(-1).astype(np.int64)


def relu(v):
    return np.maximum(v, 0.0)


K, T, D, V, H, N = 1024, 1024, 4, 512, 1024, 128
P = 2 ** 7


def setup_inputs():
    n = np.random.standard_normal
    s = mx_kscale(K)[:, None]
    u = mx_kscale(H)
    return {
        "xT": (n((K, T)) * s).astype(np.float32),
        "w1": (n((K, H)) / np.sqrt(K) / s * u).astype(np.float32),
        "w2": (n((H, N)) / np.sqrt(H) / u[:, None]).astype(np.float32),
        "gate": np.tile(np.random.uniform(0.2, 1.0, (D, 1, V)) / np.sqrt(D), (1, P, 1)).astype(np.float32),
        "pos1": striped(np.random.permutation(T)[:V]),
        "pos2": striped(np.random.permutation(T)[:V]),
        "pos3": striped(np.random.permutation(T)[:V]),
        "pos4": striped(np.random.permutation(T)[:V]),
    }


def reference(xT, w1, w2, gate, pos1, pos2, pos3, pos4):
    h = relu(mxq(f64(w1), 0, "e4m3").T @ mxq(f64(xT), 0, "e4m3"))
    z = sum(f64(gate)[d, :1] * h[:, unstriped(p)] for d, p in enumerate((pos1, pos2, pos3, pos4)))
    return mxq(f64(w2), 0, "e4m3").T @ mxq(z, 0, "e4m3")

@@ -1,0 +1,220 @@
+from contextlib import ExitStack
+
+import concourse.mybir as mybir
+from concourse.masks import make_identity
+
+K, T, D, V, H, N = 1024, 1024, 4, 512, 1024, 128
+FLOPS = 2 * K * T * H + 2 * H * V * N
+
+F32 = mybir.dt.float32
+BF16 = mybir.dt.bfloat16
+U32 = mybir.dt.uint32
+U16 = mybir.dt.uint16
+U8 = mybir.dt.uint8
+FP8X4 = mybir.dt.float8_e4m3fn_x4
+MULT = mybir.AluOpType.mult
+RELU = mybir.ActivationFunctionType.Relu
+
+P = 128
+PACK = 4
+K_PASS = P * PACK
+PASSES = K // K_PASS
+BLOCKS = H // P
+VB = V // P
+
+
+def tile_picked_gcn_mlp_relu_sub_l_kernel(tc, xT, w1, w2, gate, pos1, pos2, pos3, pos4, out):
+    nc = tc.nc
+    with ExitStack() as ctx:
+        keep = ctx.enter_context(tc.tile_pool(name="keep", bufs=1))
+        hpool = ctx.enter_context(tc.tile_pool(name="hpool", bufs=3))
+        gpool = ctx.enter_context(tc.tile_pool(name="gpool", bufs=8))
+        ps_h = ctx.enter_context(tc.psum_pool(name="ps_h", bufs=3))
+        ps_z = ctx.enter_context(tc.psum_pool(name="ps_z", bufs=2))
+        ps_t = ctx.enter_context(tc.psum_pool(name="ps_t", bufs=2))
+        ps_o = ctx.enter_context(tc.psum_pool(name="ps_o", bufs=1))
+
+        lists = [keep.tile([P, V // 16], U16, name=f"list{d}") for d in range(D)]
+        gates = keep.tile([P, D, V], F32, name="gates")
+        ident = keep.tile([P, P], F32, name="ident")
+        make_identity(nc, ident[:])
+
+        def load_rows(dst, src, g, cols):
+            nc.sync.dma_start(out=dst, in_=src[g * K_PASS : (g + 1) * K_PASS, cols].rearrange("(p j) c -> p j c", j=PACK))
+
+        w1_loads = [(0, 128), (128, 256), (256, 512), (512, 1024)]
+        w1_raw = [keep.tile([P, PASSES, PACK, b - a], F32, name=f"w1_raw{a}") for a, b in w1_loads]
+        x_loads = [(0, 0, 512), (1, 0, 512), (0, 512, 1024), (1, 512, 768), (1, 768, 1024)]
+        x_raw = [keep.tile([P, PACK, b - a], F32, name=f"x_raw{g}_{a}") for g, a, b in x_loads]
+        w2_raw = keep.tile([P, PASSES, PACK, N], F32, name="w2_raw")
+
+        def load_w1(n):
+            a, b = w1_loads[n]
+            for g in range(PASSES):
+                load_rows(w1_raw[n][:, g], w1, g, slice(a, b))
+
+        def load_x(n):
+            g, a, b = x_loads[n]
+            load_rows(x_raw[n][:], xT, g, slice(a, b))
+
+        load_w1(0)
+        load_x(0)
+        load_x(1)
+        for tile, src in zip(lists, (pos1, pos2, pos3, pos4)):
+            nc.sync.dma_start(tile[:], src)
+        load_x(2)
+        load_x(3)
+        load_x(4)
+        for d in range(D):
+            nc.sync.dma_start(out=gates[:, d, :], in_=gate[d])
+        load_w1(1)
+        load_w1(2)
+        load_w1(3)
+        for g in range(PASSES):
+            load_rows(w2_raw[:, g], w2, g, slice(0, N))
+
+        x_codes = keep.tile([P, PASSES, T], U32, align_bytes=64, name="x_codes")
+        x_scales = keep.tile([P, PASSES, T], U8, align_bytes=64, name="x_scales")
+        w1_codes = [keep.tile([P, PASSES, P], U32, align_bytes=64, name=f"w1_codes{b}") for b in range(BLOCKS)]
+        w1_scales = [keep.tile([P, PASSES, P], U8, align_bytes=64, name=f"w1_scales{b}") for b in range(BLOCKS)]
+        w2_codes = keep.tile([P, PASSES, N], U32, align_bytes=64, name="w2_codes")
+        w2_scales = keep.tile([P, PASSES, N], U8, align_bytes=64, name="w2_scales")
+        z_codes = keep.tile([P, PASSES, V], U32, align_bytes=64, name="z_codes")
+        z_scales = keep.tile([P, PASSES, V], U8, align_bytes=64, name="z_scales")
+
+        def quantize(codes, scales, grouped):
+            nc.vector.quantize_mx(out=codes.bitcast(FP8X4), scales=scales, in_=grouped)
+
+        def prepare_w1(b, on_vector):
+            n = max(i for i, (a, e) in enumerate(w1_loads) if a <= b * P)
+            c = b * P - w1_loads[n][0]
+            grouped = keep.tile([P, PASSES, P, PACK], BF16, align_bytes=64, name=f"w1_grouped{b}")
+            src = w1_raw[n][:, :, :, c : c + P].rearrange("p g j c -> p g c j")
+            if on_vector:
+                nc.vector.tensor_copy(out=grouped[:], in_=src)
+            else:
+                nc.scalar.copy(out=grouped[:], in_=src)
+            quantize(
+                w1_codes[b][:].rearrange("p g c -> p (g c)"),
+                w1_scales[b][:].rearrange("p g c -> p (g c)"),
+                grouped[:].rearrange("p g c j -> p (g c j)"),
+            )
+
+        def prepare_x(n, parts):
+            g, a, b = x_loads[n]
+            done = []
+            for c0, c1, eng in parts:
+                grouped = keep.tile([P, c1 - c0, PACK], BF16, align_bytes=64, name=f"x_grouped{n}_{c0}")
+                src = x_raw[n][:, :, c0:c1].rearrange("p j c -> p c j")
+                if eng == "v":
+                    nc.vector.tensor_copy(out=grouped[:], in_=src)
+                else:
+                    nc.scalar.copy(out=grouped[:], in_=src)
+                done.append((c0, c1, grouped))
+            for c0, c1, grouped in done:
+                quantize(x_codes[:, g, a + c0 : a + c1], x_scales[:, g, a + c0 : a + c1], grouped[:].rearrange("p c j -> p (c j)"))
+
+        def project(b, ranges, h):
+            for a, e, pieces in ranges:
+                bank = ps_h.tile([P, 512], F32, name="h_bank")
+                for pa, pe in pieces:
+                    for g in range(PASSES):
+                        nc.tensor.matmul_mx(
+                            out=bank[:, pa - a : pe - a],
+                            lhsT=w1_codes[b][:, g, :].bitcast(FP8X4),
+                            lhsT_scale=w1_scales[b][:, g, :],
+                            rhs=x_codes[:, g, pa:pe].bitcast(FP8X4),
+                            rhs_scale=x_scales[:, g, pa:pe],
+                            start=(g == 0),
+                            stop=(g == PASSES - 1),
+                        )
+                    nc.scalar.activation(h[:, pa:pe], bank[:, pa - a : pe - a], RELU)
+
+        zT = keep.tile([P, VB, H], BF16, name="zT")
+        zT_words = zT[:].rearrange("p v i -> p (v i)").bitcast(F32)
+
+        def gather(b, h, v0, v1):
+            picked = []
+            for d in range(D):
+                g = gpool.tile([P, V], F32, name="picked")
+                nc.vector.tensor_tensor(
+                    g[:, : v1 - v0], h[:].indirect(lists[d][:, v0 // 16 : v1 // 16]), gates[:, d, v0:v1], MULT
+                )
+                picked.append(g)
+            return picked
+
+        def add_up(b, picked, v0, v1):
+            n = (v1 - v0) // P
+            bank = ps_z.tile([P, VB, P], F32, name="z_bank")
+            for q in range(n):
+                for d in range(D):
+                    nc.tensor.matmul(
+                        bank[:, q, :], picked[d][:, q * P : (q + 1) * P], ident[:],
+                        start=(d == 0), stop=(d == D - 1), is_transpose=True,
+                    )
+            nc.scalar.copy(out=zT[:, v0 // P : v1 // P, b * P : (b + 1) * P], in_=bank[:, :n, :])
+
+        def turn_back(g, v0, v1):
+            grouped = keep.tile([P, (v1 - v0), PACK], BF16, align_bytes=64, name=f"z_grouped{g}_{v0}")
+            words = grouped[:].rearrange("p v t -> p (v t)").bitcast(F32).rearrange("p (v r u) -> p v r u", r=P, u=2)
+            for q0 in range(v0 // P, v1 // P, 2):
+                bank = ps_t.tile([P, 2, 2, P], F32, name="t_bank")
+                for q in (q0, q0 + 1):
+                    for u in range(2):
+                        at = q * (H // 2) + g * (K_PASS // 2) + u
+                        nc.tensor.transpose(bank[:, q - q0, u, :], zT_words[:, at : at + 2 * P - 1 : 2], ident[:])
+                r0 = q0 - v0 // P
+                nc.scalar.copy(out=words[:, r0 : r0 + 2], in_=bank[:].rearrange("p q u r -> p q r u"))
+            quantize(z_codes[:, g, v0:v1], z_scales[:, g, v0:v1], grouped[:].rearrange("p v t -> p (v t)"))
+
+        def finish(v0, v1):
+            bank = ps_o.tile([P, V], F32, name="o_bank")
+            for g in range(PASSES):
+                nc.tensor.matmul_mx(
+                    out=bank[:, : v1 - v0],
+                    lhsT=w2_codes[:, g, :].bitcast(FP8X4),
+                    lhsT_scale=w2_scales[:, g, :],
+                    rhs=z_codes[:, g, v0:v1].bitcast(FP8X4),
+                    rhs_scale=z_scales[:, g, v0:v1],
+                    start=(g == 0),
+                    stop=(g == PASSES - 1),
+                )
+            result = keep.tile([P, v1 - v0], F32, name=f"result{v0}")
+            nc.scalar.copy(out=result[:], in_=bank[:, : v1 - v0])
+            nc.sync.dma_start(out=out[:, v0:v1], in_=result[:])
+
+        prepare_w1(0, True)
+        halves = ((0, 256, "v"), (256, 512, "s"))
+        prepare_x(0, halves)
+        prepare_x(1, halves)
+        prepare_x(2, halves)
+        prepare_x(3, ((0, 128, "v"), (128, 256, "s")))
+        prepare_x(4, ((0, 128, "v"), (128, 256, "s")))
+        h = hpool.tile([P, T], F32, name="h")
+        project(0, ((0, 512, ((0, 512),)), (512, 1024, ((512, 768), (768, 1024)))), h)
+        whole = ((0, 512, ((0, 512),)), (512, 1024, ((512, 1024),)))
+        prepare_w1(1, False)
+        for b in range(BLOCKS):
+            if b + 1 < BLOCKS:
+                h_next = hpool.tile([P, T], F32, name="h")
+                project(b + 1, whole, h_next)
+            if b + 2 < BLOCKS:
+                prepare_w1(b + 2, False)
+            if b == 5:
+                w2_grouped = keep.tile([P, PASSES, N, PACK], BF16, align_bytes=64, name="w2_grouped")
+                nc.scalar.copy(out=w2_grouped[:], in_=w2_raw[:].rearrange("p g j c -> p g c j"))
+                quantize(
+                    w2_codes[:].rearrange("p g c -> p (g c)"),
+                    w2_scales[:].rearrange("p g c -> p (g c)"),
+                    w2_grouped[:].rearrange("p g c j -> p (g c j)"),
+                )
+            for v0, v1 in ((0, V),) if b + 1 < BLOCKS else ((0, V // 2), (V // 2, V)):
+                picked = gather(b, h, v0, v1)
+                add_up(b, picked, v0, v1)
+                if b == BLOCKS - 1:
+                    turn_back(1, v0, v1)
+                    finish(v0, v1)
+            if b == BLOCKS // 2 - 1:
+                turn_back(0, 0, V)
+            if b + 1 < BLOCKS:
+                h = h_next

@@ -27,12 +27,11 @@ def tile_picked_gcn_mlp_relu_sub_l_kernel(tc, xT, w1, w2, gate, pos1, pos2, pos3
     nc = tc.nc
     with ExitStack() as ctx:
         keep = ctx.enter_context(tc.tile_pool(name="keep", bufs=1))
-        hpool = ctx.enter_context(tc.tile_pool(name="hpool", bufs=3))
-        gpool = ctx.enter_context(tc.tile_pool(name="gpool", bufs=8))
+        hpool = ctx.enter_context(tc.tile_pool(name="hpool", bufs=4))
+        gpool = ctx.enter_context(tc.tile_pool(name="gpool", bufs=12))
         ps_h = ctx.enter_context(tc.psum_pool(name="ps_h", bufs=3))
-        ps_z = ctx.enter_context(tc.psum_pool(name="ps_z", bufs=2))
+        ps_z = ctx.enter_context(tc.psum_pool(name="ps_z", bufs=3))
         ps_t = ctx.enter_context(tc.psum_pool(name="ps_t", bufs=2))
-        ps_o = ctx.enter_context(tc.psum_pool(name="ps_o", bufs=1))
 
         lists = [keep.tile([P, V // 16], U16, name=f"list{d}") for d in range(D)]
         gates = keep.tile([P, D, V], F32, name="gates")
@@ -43,8 +42,9 @@ def tile_picked_gcn_mlp_relu_sub_l_kernel(tc, xT, w1, w2, gate, pos1, pos2, pos3
             nc.sync.dma_start(out=dst, in_=src[g * K_PASS : (g + 1) * K_PASS, cols].rearrange("(p j) c -> p j c", j=PACK))
 
         w1_loads = [(0, 128), (128, 256), (256, 512), (512, 1024)]
+        w1_parts = [(b * P, (b + 1) * P) for b in range(BLOCKS)]
         w1_raw = [keep.tile([P, PASSES, PACK, b - a], F32, name=f"w1_raw{a}") for a, b in w1_loads]
-        x_loads = [(0, 0, 512), (1, 0, 512), (0, 512, 1024), (1, 512, 768), (1, 768, 1024)]
+        x_loads = [(0, 0, 512), (1, 0, 512), (0, 512, 1024), (1, 512, 768), (1, 768, 896), (1, 896, 1024)]
         x_raw = [keep.tile([P, PACK, b - a], F32, name=f"x_raw{g}_{a}") for g, a, b in x_loads]
         w2_raw = keep.tile([P, PASSES, PACK, N], F32, name="w2_raw")
 
@@ -60,14 +60,15 @@ def tile_picked_gcn_mlp_relu_sub_l_kernel(tc, xT, w1, w2, gate, pos1, pos2, pos3
         load_w1(0)
         load_x(0)
         load_x(1)
-        for tile, src in zip(lists, (pos1, pos2, pos3, pos4)):
-            nc.sync.dma_start(tile[:], src)
         load_x(2)
         load_x(3)
         load_x(4)
-        for d in range(D):
+        load_x(5)
+        for d, src in enumerate((pos1, pos2, pos3, pos4)):
+            nc.sync.dma_start(lists[d][:], src)
             nc.sync.dma_start(out=gates[:, d, :], in_=gate[d])
-        load_w1(1)
+            if d == 1:
+                load_w1(1)
         load_w1(2)
         load_w1(3)
         for g in range(PASSES):
@@ -75,8 +76,8 @@ def tile_picked_gcn_mlp_relu_sub_l_kernel(tc, xT, w1, w2, gate, pos1, pos2, pos3
 
         x_codes = keep.tile([P, PASSES, T], U32, align_bytes=64, name="x_codes")
         x_scales = keep.tile([P, PASSES, T], U8, align_bytes=64, name="x_scales")
-        w1_codes = [keep.tile([P, PASSES, P], U32, align_bytes=64, name=f"w1_codes{b}") for b in range(BLOCKS)]
-        w1_scales = [keep.tile([P, PASSES, P], U8, align_bytes=64, name=f"w1_scales{b}") for b in range(BLOCKS)]
+        w1_codes = [keep.tile([P, PASSES, e - a], U32, align_bytes=64, name=f"w1_codes{a}") for a, e in w1_parts]
+        w1_scales = [keep.tile([P, PASSES, e - a], U8, align_bytes=64, name=f"w1_scales{a}") for a, e in w1_parts]
         w2_codes = keep.tile([P, PASSES, N], U32, align_bytes=64, name="w2_codes")
         w2_scales = keep.tile([P, PASSES, N], U8, align_bytes=64, name="w2_scales")
         z_codes = keep.tile([P, PASSES, V], U32, align_bytes=64, name="z_codes")
@@ -85,63 +86,73 @@ def tile_picked_gcn_mlp_relu_sub_l_kernel(tc, xT, w1, w2, gate, pos1, pos2, pos3
         def quantize(codes, scales, grouped):
             nc.vector.quantize_mx(out=codes.bitcast(FP8X4), scales=scales, in_=grouped)
 
-        def prepare_w1(b, on_vector):
-            n = max(i for i, (a, e) in enumerate(w1_loads) if a <= b * P)
-            c = b * P - w1_loads[n][0]
-            grouped = keep.tile([P, PASSES, P, PACK], BF16, align_bytes=64, name=f"w1_grouped{b}")
-            src = w1_raw[n][:, :, :, c : c + P].rearrange("p g j c -> p g c j")
+        def prepare_w1(part, on_vector):
+            a, e = w1_parts[part]
+            n = max(i for i, (la, le) in enumerate(w1_loads) if la <= a)
+            c = a - w1_loads[n][0]
+            grouped = keep.tile([P, PASSES, e - a, PACK], BF16, align_bytes=64, name=f"stage{part}")
+            src = w1_raw[n][:, :, :, c : c + e - a].rearrange("p g j c -> p g c j")
             if on_vector:
                 nc.vector.tensor_copy(out=grouped[:], in_=src)
             else:
                 nc.scalar.copy(out=grouped[:], in_=src)
             quantize(
-                w1_codes[b][:].rearrange("p g c -> p (g c)"),
-                w1_scales[b][:].rearrange("p g c -> p (g c)"),
+                w1_codes[part][:].rearrange("p g c -> p (g c)"),
+                w1_scales[part][:].rearrange("p g c -> p (g c)"),
                 grouped[:].rearrange("p g c j -> p (g c j)"),
             )
 
-        def prepare_x(n, parts):
+        def copy_x(n, c0, c1, eng, tile=None, t0=None):
             g, a, b = x_loads[n]
-            done = []
-            for c0, c1, eng in parts:
-                grouped = keep.tile([P, c1 - c0, PACK], BF16, align_bytes=64, name=f"x_grouped{n}_{c0}")
-                src = x_raw[n][:, :, c0:c1].rearrange("p j c -> p c j")
-                if eng == "v":
-                    nc.vector.tensor_copy(out=grouped[:], in_=src)
-                else:
-                    nc.scalar.copy(out=grouped[:], in_=src)
-                done.append((c0, c1, grouped))
-            for c0, c1, grouped in done:
-                quantize(x_codes[:, g, a + c0 : a + c1], x_scales[:, g, a + c0 : a + c1], grouped[:].rearrange("p c j -> p (c j)"))
+            if tile is None:
+                tile, t0 = keep.tile([P, c1 - c0, PACK], BF16, align_bytes=64, name=f"x_grouped{n}_{c0}"), c0
+            src = x_raw[n][:, :, c0:c1].rearrange("p j c -> p c j")
+            if eng == "v":
+                nc.vector.tensor_copy(out=tile[:, c0 - t0 : c1 - t0], in_=src)
+            else:
+                nc.scalar.copy(out=tile[:, c0 - t0 : c1 - t0], in_=src)
+            return tile
 
-        def project(b, ranges, h):
+        def quantize_x(n, c0, c1, tile):
+            g, a, b = x_loads[n]
+            quantize(x_codes[:, g, a + c0 : a + c1], x_scales[:, g, a + c0 : a + c1], tile[:].rearrange("p c j -> p (c j)"))
+
+        def relu(dst, src, on_vector):
+            if on_vector:
+                nc.vector.tensor_scalar_max(dst, src, 0.0)
+            else:
+                nc.scalar.activation(dst, src, RELU)
+
+        def project(b, ranges, h, last_on_vector=None):
+            part = max(i for i, (pa, pe) in enumerate(w1_parts) if pa <= b * P)
+            c = b * P - w1_parts[part][0]
             for a, e, pieces in ranges:
                 bank = ps_h.tile([P, 512], F32, name="h_bank")
                 for pa, pe in pieces:
                     for g in range(PASSES):
                         nc.tensor.matmul_mx(
                             out=bank[:, pa - a : pe - a],
-                            lhsT=w1_codes[b][:, g, :].bitcast(FP8X4),
-                            lhsT_scale=w1_scales[b][:, g, :],
+                            lhsT=w1_codes[part][:, g, c : c + P].bitcast(FP8X4),
+                            lhsT_scale=w1_scales[part][:, g, c : c + P],
                             rhs=x_codes[:, g, pa:pe].bitcast(FP8X4),
                             rhs_scale=x_scales[:, g, pa:pe],
                             start=(g == 0),
                             stop=(g == PASSES - 1),
                         )
-                    nc.scalar.activation(h[:, pa:pe], bank[:, pa - a : pe - a], RELU)
+                    relu(h[:, pa:pe], bank[:, pa - a : pe - a], pa == last_on_vector)
 
         zT = keep.tile([P, VB, H], BF16, name="zT")
         zT_words = zT[:].rearrange("p v i -> p (v i)").bitcast(F32)
 
-        def gather(b, h, v0, v1):
-            picked = []
-            for d in range(D):
+        behind = {(0, 1): 1, (1, 1): 2, (1, 2): 3, (2, 2): 4, (2, 3): 5, (3, 2): 6, (4, 2): 7}
+
+        def gather(b, d, v0, v1):
+            if (b, d) in behind and v0 == 0:
+                g = keep.tile([P, V], F32, align_bytes=64, name=f"stage{behind[b, d]}")
+            else:
                 g = gpool.tile([P, V], F32, name="picked")
-                nc.vector.tensor_tensor(
-                    g[:, : v1 - v0], h[:].indirect(lists[d][:, v0 // 16 : v1 // 16]), gates[:, d, v0:v1], MULT
-                )
-                picked.append(g)
-            return picked
+            nc.vector.tensor_tensor(g[:, : v1 - v0], hs[b][:].indirect(lists[d][:, v0 // 16 : v1 // 16]), gates[:, d, v0:v1], MULT)
+            return g
 
         def add_up(b, picked, v0, v1):
             n = (v1 - v0) // P
@@ -154,21 +165,26 @@ def tile_picked_gcn_mlp_relu_sub_l_kernel(tc, xT, w1, w2, gate, pos1, pos2, pos3
                     )
             nc.scalar.copy(out=zT[:, v0 // P : v1 // P, b * P : (b + 1) * P], in_=bank[:, :n, :])
 
-        def turn_back(g, v0, v1):
+        def turn_back(g, v0, v1, on_vector=False):
             grouped = keep.tile([P, (v1 - v0), PACK], BF16, align_bytes=64, name=f"z_grouped{g}_{v0}")
             words = grouped[:].rearrange("p v t -> p (v t)").bitcast(F32).rearrange("p (v r u) -> p v r u", r=P, u=2)
             for q0 in range(v0 // P, v1 // P, 2):
+                n = min(2, v1 // P - q0)
                 bank = ps_t.tile([P, 2, 2, P], F32, name="t_bank")
-                for q in (q0, q0 + 1):
+                for q in range(q0, q0 + n):
                     for u in range(2):
                         at = q * (H // 2) + g * (K_PASS // 2) + u
                         nc.tensor.transpose(bank[:, q - q0, u, :], zT_words[:, at : at + 2 * P - 1 : 2], ident[:])
                 r0 = q0 - v0 // P
-                nc.scalar.copy(out=words[:, r0 : r0 + 2], in_=bank[:].rearrange("p q u r -> p q r u"))
+                copy = nc.vector.tensor_copy if on_vector else nc.scalar.copy
+                copy(out=words[:, r0 : r0 + n], in_=bank[:, :n].rearrange("p q u r -> p q r u"))
+            return grouped
+
+        def quantize_z(g, v0, v1, grouped):
             quantize(z_codes[:, g, v0:v1], z_scales[:, g, v0:v1], grouped[:].rearrange("p v t -> p (v t)"))
 
-        def finish(v0, v1):
-            bank = ps_o.tile([P, V], F32, name="o_bank")
+        def multiply(v0, v1):
+            bank = ps_h.tile([P, V], F32, name="h_bank")
             for g in range(PASSES):
                 nc.tensor.matmul_mx(
                     out=bank[:, : v1 - v0],
@@ -179,42 +195,68 @@ def tile_picked_gcn_mlp_relu_sub_l_kernel(tc, xT, w1, w2, gate, pos1, pos2, pos3
                     start=(g == 0),
                     stop=(g == PASSES - 1),
                 )
+            return bank
+
+        def store(v0, v1, bank, on_vector):
             result = keep.tile([P, v1 - v0], F32, name=f"result{v0}")
-            nc.scalar.copy(out=result[:], in_=bank[:, : v1 - v0])
+            if on_vector:
+                nc.vector.tensor_copy(out=result[:], in_=bank[:, : v1 - v0])
+            else:
+                nc.scalar.copy(out=result[:], in_=bank[:, : v1 - v0])
             nc.sync.dma_start(out=out[:, v0:v1], in_=result[:])
 
+        def prepare_w2():
+            w2_grouped = keep.tile([P, PASSES, N, PACK], BF16, align_bytes=64, name="w2_grouped")
+            nc.scalar.copy(out=w2_grouped[:], in_=w2_raw[:].rearrange("p g j c -> p g c j"))
+            quantize(
+                w2_codes[:].rearrange("p g c -> p (g c)"),
+                w2_scales[:].rearrange("p g c -> p (g c)"),
+                w2_grouped[:].rearrange("p g c j -> p (g c j)"),
+            )
+
         prepare_w1(0, True)
-        halves = ((0, 256, "v"), (256, 512, "s"))
-        prepare_x(0, halves)
-        prepare_x(1, halves)
-        prepare_x(2, halves)
-        prepare_x(3, ((0, 128, "v"), (128, 256, "s")))
-        prepare_x(4, ((0, 128, "v"), (128, 256, "s")))
-        h = hpool.tile([P, T], F32, name="h")
-        project(0, ((0, 512, ((0, 512),)), (512, 1024, ((512, 768), (768, 1024)))), h)
+        hs = [hpool.tile([P, T], F32, name="h")]
+        for n, (g, a, b) in enumerate(x_loads):
+            quantize_x(n, 0, b - a, copy_x(n, 0, b - a, "v"))
+        project(0, ((0, 512, ((0, 512),)), (512, 1024, ((512, 768), (768, 896), (896, 1024)))), hs[0], last_on_vector=896)
         whole = ((0, 512, ((0, 512),)), (512, 1024, ((512, 1024),)))
-        prepare_w1(1, False)
-        for b in range(BLOCKS):
-            if b + 1 < BLOCKS:
-                h_next = hpool.tile([P, T], F32, name="h")
-                project(b + 1, whole, h_next)
-            if b + 2 < BLOCKS:
-                prepare_w1(b + 2, False)
-            if b == 5:
-                w2_grouped = keep.tile([P, PASSES, N, PACK], BF16, align_bytes=64, name="w2_grouped")
-                nc.scalar.copy(out=w2_grouped[:], in_=w2_raw[:].rearrange("p g j c -> p g c j"))
-                quantize(
-                    w2_codes[:].rearrange("p g c -> p (g c)"),
-                    w2_scales[:].rearrange("p g c -> p (g c)"),
-                    w2_grouped[:].rearrange("p g c j -> p (g c j)"),
-                )
-            for v0, v1 in ((0, V),) if b + 1 < BLOCKS else ((0, V // 2), (V // 2, V)):
-                picked = gather(b, h, v0, v1)
-                add_up(b, picked, v0, v1)
-                if b == BLOCKS - 1:
-                    turn_back(1, v0, v1)
-                    finish(v0, v1)
-            if b == BLOCKS // 2 - 1:
-                turn_back(0, 0, V)
-            if b + 1 < BLOCKS:
-                h = h_next
+        picked = []
+        for b in range(BLOCKS - 1):
+            hs.append(hpool.tile([P, T], F32, name="h"))
+            now = []
+            for d in range(D):
+                now.append(gather(b, d, 0, V))
+                if (b, d + 1) in behind:
+                    prepare_w1(behind[b, d + 1], False)
+                if (b, d) == (4, 1):
+                    prepare_w2()
+                if (b, d) == (5, 1):
+                    z0 = turn_back(0, 0, V)
+                if (b, d) == (6, 0):
+                    quantize_z(0, 0, V, z0)
+                if (b, d) in ((0, 0), (1, 0)) or (b > 1 and d == 0):
+                    project(b + 1, whole, hs[b + 1])
+                    if b > 0:
+                        add_up(b - 1, picked, 0, V)
+            picked = now
+        b = BLOCKS - 1
+        parts = ((0, 256), (256, 384), (384, 512))
+        last = [[gather(b, d, *parts[0]) for d in range(D)]]
+        add_up(b - 1, picked, 0, V)
+        for part in parts[1:]:
+            last.append([gather(b, d, *part) for d in range(D)])
+        grouped = []
+        for i in (0, 1):
+            add_up(b, last[i], *parts[i])
+            grouped.append(turn_back(1, *parts[i], on_vector=(i == 1)))
+        add_up(b, last[2], *parts[2])
+        quantize_z(1, *parts[0], grouped[0])
+        quantize_z(1, *parts[1], grouped[1])
+        bank0 = multiply(*parts[0])
+        z1 = turn_back(1, *parts[2])
+        quantize_z(1, *parts[2], z1)
+        bank1 = multiply(*parts[1])
+        bank2 = multiply(*parts[2])
+        store(*parts[0], bank0, True)
+        store(*parts[1], bank1, True)
+        store(*parts[2], bank2, False)

@@ -41,10 +41,10 @@ def tile_picked_gcn_mlp_relu_sub_l_kernel(tc, xT, w1, w2, gate, pos1, pos2, pos3
         def load_rows(dst, src, g, cols):
             nc.sync.dma_start(out=dst, in_=src[g * K_PASS : (g + 1) * K_PASS, cols].rearrange("(p j) c -> p j c", j=PACK))
 
-        w1_loads = [(0, 128), (128, 256), (256, 512), (512, 1024)]
+        w1_loads = [(0, 128), (128, 256), (256, 512), (512, 768), (768, 1024)]
         w1_parts = [(b * P, (b + 1) * P) for b in range(BLOCKS)]
         w1_raw = [keep.tile([P, PASSES, PACK, b - a], F32, name=f"w1_raw{a}") for a, b in w1_loads]
-        x_loads = [(0, 0, 512), (1, 0, 512), (0, 512, 1024), (1, 512, 768), (1, 768, 896), (1, 896, 1024)]
+        x_loads = [(0, 0, 512), (1, 0, 512), (0, 512, 1024), (1, 512, 768), (1, 768, 1024)]
         x_raw = [keep.tile([P, PACK, b - a], F32, name=f"x_raw{g}_{a}") for g, a, b in x_loads]
         w2_raw = keep.tile([P, PASSES, PACK, N], F32, name="w2_raw")
 
@@ -58,19 +58,15 @@ def tile_picked_gcn_mlp_relu_sub_l_kernel(tc, xT, w1, w2, gate, pos1, pos2, pos3
             load_rows(x_raw[n][:], xT, g, slice(a, b))
 
         load_w1(0)
-        load_x(0)
-        load_x(1)
-        load_x(2)
-        load_x(3)
-        load_x(4)
-        load_x(5)
+        for n in range(len(x_loads)):
+            load_x(n)
+        load_w1(1)
         for d, src in enumerate((pos1, pos2, pos3, pos4)):
             nc.sync.dma_start(lists[d][:], src)
             nc.sync.dma_start(out=gates[:, d, :], in_=gate[d])
-            if d == 1:
-                load_w1(1)
         load_w1(2)
         load_w1(3)
+        load_w1(4)
         for g in range(PASSES):
             load_rows(w2_raw[:, g], w2, g, slice(0, N))
 
@@ -90,7 +86,7 @@ def tile_picked_gcn_mlp_relu_sub_l_kernel(tc, xT, w1, w2, gate, pos1, pos2, pos3
             a, e = w1_parts[part]
             n = max(i for i, (la, le) in enumerate(w1_loads) if la <= a)
             c = a - w1_loads[n][0]
-            grouped = keep.tile([P, PASSES, e - a, PACK], BF16, align_bytes=64, name=f"stage{part}")
+            grouped = keep.tile([P, PASSES, e - a, PACK], BF16, align_bytes=64, name=f"stage{part % 2}" if part else "stage_first")
             src = w1_raw[n][:, :, :, c : c + e - a].rearrange("p g j c -> p g c j")
             if on_vector:
                 nc.vector.tensor_copy(out=grouped[:], in_=src)
@@ -144,11 +140,11 @@ def tile_picked_gcn_mlp_relu_sub_l_kernel(tc, xT, w1, w2, gate, pos1, pos2, pos3
         zT = keep.tile([P, VB, H], BF16, name="zT")
         zT_words = zT[:].rearrange("p v i -> p (v i)").bitcast(F32)
 
-        behind = {(0, 1): 1, (1, 1): 2, (1, 2): 3, (2, 2): 4, (2, 3): 5, (3, 2): 6, (4, 2): 7}
+        behind = {(0, 1): 1, (1, 1): 2, (1, 2): 3, (2, 2): 4, (3, 1): 5, (4, 1): 6, (5, 1): 7}
 
         def gather(b, d, v0, v1):
             if (b, d) in behind and v0 == 0:
-                g = keep.tile([P, V], F32, align_bytes=64, name=f"stage{behind[b, d]}")
+                g = keep.tile([P, V], F32, align_bytes=64, name=f"stage{behind[b, d] % 2}")
             else:
                 g = gpool.tile([P, V], F32, name="picked")
             nc.vector.tensor_tensor(g[:, : v1 - v0], hs[b][:].indirect(lists[d][:, v0 // 16 : v1 // 16]), gates[:, d, v0:v1], MULT)
@@ -165,7 +161,7 @@ def tile_picked_gcn_mlp_relu_sub_l_kernel(tc, xT, w1, w2, gate, pos1, pos2, pos3
                     )
             nc.scalar.copy(out=zT[:, v0 // P : v1 // P, b * P : (b + 1) * P], in_=bank[:, :n, :])
 
-        def turn_back(g, v0, v1, on_vector=False):
+        def turn_back(g, v0, v1):
             grouped = keep.tile([P, (v1 - v0), PACK], BF16, align_bytes=64, name=f"z_grouped{g}_{v0}")
             words = grouped[:].rearrange("p v t -> p (v t)").bitcast(F32).rearrange("p (v r u) -> p v r u", r=P, u=2)
             for q0 in range(v0 // P, v1 // P, 2):
@@ -176,8 +172,7 @@ def tile_picked_gcn_mlp_relu_sub_l_kernel(tc, xT, w1, w2, gate, pos1, pos2, pos3
                         at = q * (H // 2) + g * (K_PASS // 2) + u
                         nc.tensor.transpose(bank[:, q - q0, u, :], zT_words[:, at : at + 2 * P - 1 : 2], ident[:])
                 r0 = q0 - v0 // P
-                copy = nc.vector.tensor_copy if on_vector else nc.scalar.copy
-                copy(out=words[:, r0 : r0 + n], in_=bank[:, :n].rearrange("p q u r -> p q r u"))
+                nc.scalar.copy(out=words[:, r0 : r0 + n], in_=bank[:, :n].rearrange("p q u r -> p q r u"))
             return grouped
 
         def quantize_z(g, v0, v1, grouped):
@@ -218,7 +213,7 @@ def tile_picked_gcn_mlp_relu_sub_l_kernel(tc, xT, w1, w2, gate, pos1, pos2, pos3
         hs = [hpool.tile([P, T], F32, name="h")]
         for n, (g, a, b) in enumerate(x_loads):
             quantize_x(n, 0, b - a, copy_x(n, 0, b - a, "v"))
-        project(0, ((0, 512, ((0, 512),)), (512, 1024, ((512, 768), (768, 896), (896, 1024)))), hs[0], last_on_vector=896)
+        project(0, ((0, 512, ((0, 512),)), (512, 1024, ((512, 768), (768, 1024)))), hs[0], last_on_vector=768)
         whole = ((0, 512, ((0, 512),)), (512, 1024, ((512, 1024),)))
         picked = []
         for b in range(BLOCKS - 1):
@@ -228,13 +223,13 @@ def tile_picked_gcn_mlp_relu_sub_l_kernel(tc, xT, w1, w2, gate, pos1, pos2, pos3
                 now.append(gather(b, d, 0, V))
                 if (b, d + 1) in behind:
                     prepare_w1(behind[b, d + 1], False)
-                if (b, d) == (4, 1):
+                if (b, d) == (5, 2):
                     prepare_w2()
                 if (b, d) == (5, 1):
                     z0 = turn_back(0, 0, V)
-                if (b, d) == (6, 0):
+                if (b, d) == (6, 1):
                     quantize_z(0, 0, V, z0)
-                if (b, d) in ((0, 0), (1, 0)) or (b > 1 and d == 0):
+                if d == 0:
                     project(b + 1, whole, hs[b + 1])
                     if b > 0:
                         add_up(b - 1, picked, 0, V)
@@ -245,16 +240,16 @@ def tile_picked_gcn_mlp_relu_sub_l_kernel(tc, xT, w1, w2, gate, pos1, pos2, pos3
         add_up(b - 1, picked, 0, V)
         for part in parts[1:]:
             last.append([gather(b, d, *part) for d in range(D)])
-        grouped = []
-        for i in (0, 1):
-            add_up(b, last[i], *parts[i])
-            grouped.append(turn_back(1, *parts[i], on_vector=(i == 1)))
+        add_up(b, last[0], *parts[0])
+        zA = turn_back(1, *parts[0])
+        add_up(b, last[1], *parts[1])
+        quantize_z(1, *parts[0], zA)
         add_up(b, last[2], *parts[2])
-        quantize_z(1, *parts[0], grouped[0])
-        quantize_z(1, *parts[1], grouped[1])
+        zB = turn_back(1, *parts[1])
+        quantize_z(1, *parts[1], zB)
         bank0 = multiply(*parts[0])
-        z1 = turn_back(1, *parts[2])
-        quantize_z(1, *parts[2], z1)
+        zC = turn_back(1, *parts[2])
+        quantize_z(1, *parts[2], zC)
         bank1 = multiply(*parts[1])
         bank2 = multiply(*parts[2])
         store(*parts[0], bank0, True)

from contextlib import ExitStack

import concourse.mybir as mybir
from concourse.masks import make_identity

K, T, D, V, H, N = 1024, 1024, 4, 512, 1024, 128
FLOPS = 2 * K * T * H + 2 * H * V * N

F32 = mybir.dt.float32
BF16 = mybir.dt.bfloat16
U32 = mybir.dt.uint32
U16 = mybir.dt.uint16
U8 = mybir.dt.uint8
FP8X4 = mybir.dt.float8_e4m3fn_x4
MULT = mybir.AluOpType.mult
RELU = mybir.ActivationFunctionType.Relu

P = 128
PACK = 4
K_PASS = P * PACK
PASSES = K // K_PASS
BLOCKS = H // P
VB = V // P


def tile_picked_gcn_mlp_relu_sub_l_kernel(tc, xT, w1, w2, gate, pos1, pos2, pos3, pos4, out):
    nc = tc.nc
    with ExitStack() as ctx:
        keep = ctx.enter_context(tc.tile_pool(name="keep", bufs=1))
        hpool = ctx.enter_context(tc.tile_pool(name="hpool", bufs=4))
        gpool = ctx.enter_context(tc.tile_pool(name="gpool", bufs=12))
        ps_h = ctx.enter_context(tc.psum_pool(name="ps_h", bufs=3))
        ps_z = ctx.enter_context(tc.psum_pool(name="ps_z", bufs=3))
        ps_t = ctx.enter_context(tc.psum_pool(name="ps_t", bufs=2))

        lists = [keep.tile([P, V // 16], U16, name=f"list{d}") for d in range(D)]
        gates = keep.tile([P, D, V], F32, name="gates")
        ident = keep.tile([P, P], F32, name="ident")
        make_identity(nc, ident[:])

        def load_rows(dst, src, g, cols):
            nc.sync.dma_start(out=dst, in_=src[g * K_PASS : (g + 1) * K_PASS, cols].rearrange("(p j) c -> p j c", j=PACK))

        w1_loads = [(0, 128), (128, 256), (256, 512), (512, 768), (768, 1024)]
        w1_parts = [(b * P, (b + 1) * P) for b in range(BLOCKS)]
        w1_raw = [keep.tile([P, PASSES, PACK, b - a], F32, name=f"w1_raw{a}") for a, b in w1_loads]
        x_loads = [(0, 0, 512), (1, 0, 512), (0, 512, 1024), (1, 512, 768), (1, 768, 1024)]
        x_raw = [keep.tile([P, PACK, b - a], F32, name=f"x_raw{g}_{a}") for g, a, b in x_loads]
        w2_raw = keep.tile([P, PASSES, PACK, N], F32, name="w2_raw")

        def load_w1(n):
            a, b = w1_loads[n]
            for g in range(PASSES):
                load_rows(w1_raw[n][:, g], w1, g, slice(a, b))

        def load_x(n):
            g, a, b = x_loads[n]
            load_rows(x_raw[n][:], xT, g, slice(a, b))

        load_w1(0)
        for n in range(len(x_loads)):
            load_x(n)
        load_w1(1)
        for d, src in enumerate((pos1, pos2, pos3, pos4)):
            nc.sync.dma_start(lists[d][:], src)
            nc.sync.dma_start(out=gates[:, d, :], in_=gate[d])
        load_w1(2)
        load_w1(3)
        load_w1(4)
        for g in range(PASSES):
            load_rows(w2_raw[:, g], w2, g, slice(0, N))

        x_codes = keep.tile([P, PASSES, T], U32, align_bytes=64, name="x_codes")
        x_scales = keep.tile([P, PASSES, T], U8, align_bytes=64, name="x_scales")
        w1_codes = [keep.tile([P, PASSES, e - a], U32, align_bytes=64, name=f"w1_codes{a}") for a, e in w1_parts]
        w1_scales = [keep.tile([P, PASSES, e - a], U8, align_bytes=64, name=f"w1_scales{a}") for a, e in w1_parts]
        w2_codes = keep.tile([P, PASSES, N], U32, align_bytes=64, name="w2_codes")
        w2_scales = keep.tile([P, PASSES, N], U8, align_bytes=64, name="w2_scales")
        z_codes = keep.tile([P, PASSES, V], U32, align_bytes=64, name="z_codes")
        z_scales = keep.tile([P, PASSES, V], U8, align_bytes=64, name="z_scales")

        def quantize(codes, scales, grouped):
            nc.vector.quantize_mx(out=codes.bitcast(FP8X4), scales=scales, in_=grouped)

        def prepare_w1(part, on_vector):
            a, e = w1_parts[part]
            n = max(i for i, (la, le) in enumerate(w1_loads) if la <= a)
            c = a - w1_loads[n][0]
            grouped = keep.tile([P, PASSES, e - a, PACK], BF16, align_bytes=64, name=f"stage{part % 2}" if part else "stage_first")
            src = w1_raw[n][:, :, :, c : c + e - a].rearrange("p g j c -> p g c j")
            if on_vector:
                nc.vector.tensor_copy(out=grouped[:], in_=src)
            else:
                nc.scalar.copy(out=grouped[:], in_=src)
            quantize(
                w1_codes[part][:].rearrange("p g c -> p (g c)"),
                w1_scales[part][:].rearrange("p g c -> p (g c)"),
                grouped[:].rearrange("p g c j -> p (g c j)"),
            )

        def copy_x(n, c0, c1, eng, tile=None, t0=None):
            g, a, b = x_loads[n]
            if tile is None:
                tile, t0 = keep.tile([P, c1 - c0, PACK], BF16, align_bytes=64, name=f"x_grouped{n}_{c0}"), c0
            src = x_raw[n][:, :, c0:c1].rearrange("p j c -> p c j")
            if eng == "v":
                nc.vector.tensor_copy(out=tile[:, c0 - t0 : c1 - t0], in_=src)
            else:
                nc.scalar.copy(out=tile[:, c0 - t0 : c1 - t0], in_=src)
            return tile

        def quantize_x(n, c0, c1, tile):
            g, a, b = x_loads[n]
            quantize(x_codes[:, g, a + c0 : a + c1], x_scales[:, g, a + c0 : a + c1], tile[:].rearrange("p c j -> p (c j)"))

        def relu(dst, src, on_vector):
            if on_vector:
                nc.vector.tensor_scalar_max(dst, src, 0.0)
            else:
                nc.scalar.activation(dst, src, RELU)

        def project(b, ranges, h, last_on_vector=None):
            part = max(i for i, (pa, pe) in enumerate(w1_parts) if pa <= b * P)
            c = b * P - w1_parts[part][0]
            for a, e, pieces in ranges:
                bank = ps_h.tile([P, 512], F32, name="h_bank")
                for pa, pe in pieces:
                    for g in range(PASSES):
                        nc.tensor.matmul_mx(
                            out=bank[:, pa - a : pe - a],
                            lhsT=w1_codes[part][:, g, c : c + P].bitcast(FP8X4),
                            lhsT_scale=w1_scales[part][:, g, c : c + P],
                            rhs=x_codes[:, g, pa:pe].bitcast(FP8X4),
                            rhs_scale=x_scales[:, g, pa:pe],
                            start=(g == 0),
                            stop=(g == PASSES - 1),
                        )
                    relu(h[:, pa:pe], bank[:, pa - a : pe - a], pa == last_on_vector)

        zT = keep.tile([P, VB, H], BF16, name="zT")
        zT_words = zT[:].rearrange("p v i -> p (v i)").bitcast(F32)

        behind = {(0, 1): 1, (1, 1): 2, (1, 2): 3, (2, 2): 4, (3, 1): 5, (4, 1): 6, (5, 1): 7}

        def gather(b, d, v0, v1):
            if (b, d) in behind and v0 == 0:
                g = keep.tile([P, V], F32, align_bytes=64, name=f"stage{behind[b, d] % 2}")
            else:
                g = gpool.tile([P, V], F32, name="picked")
            nc.vector.tensor_tensor(g[:, : v1 - v0], hs[b][:].indirect(lists[d][:, v0 // 16 : v1 // 16]), gates[:, d, v0:v1], MULT)
            return g

        def add_up(b, picked, v0, v1):
            n = (v1 - v0) // P
            bank = ps_z.tile([P, VB, P], F32, name="z_bank")
            for q in range(n):
                for d in range(D):
                    nc.tensor.matmul(
                        bank[:, q, :], picked[d][:, q * P : (q + 1) * P], ident[:],
                        start=(d == 0), stop=(d == D - 1), is_transpose=True,
                    )
            nc.scalar.copy(out=zT[:, v0 // P : v1 // P, b * P : (b + 1) * P], in_=bank[:, :n, :])

        def turn_back(g, v0, v1):
            grouped = keep.tile([P, (v1 - v0), PACK], BF16, align_bytes=64, name=f"z_grouped{g}_{v0}")
            words = grouped[:].rearrange("p v t -> p (v t)").bitcast(F32).rearrange("p (v r u) -> p v r u", r=P, u=2)
            for q0 in range(v0 // P, v1 // P, 2):
                n = min(2, v1 // P - q0)
                bank = ps_t.tile([P, 2, 2, P], F32, name="t_bank")
                for q in range(q0, q0 + n):
                    for u in range(2):
                        at = q * (H // 2) + g * (K_PASS // 2) + u
                        nc.tensor.transpose(bank[:, q - q0, u, :], zT_words[:, at : at + 2 * P - 1 : 2], ident[:])
                r0 = q0 - v0 // P
                nc.scalar.copy(out=words[:, r0 : r0 + n], in_=bank[:, :n].rearrange("p q u r -> p q r u"))
            return grouped

        def quantize_z(g, v0, v1, grouped):
            quantize(z_codes[:, g, v0:v1], z_scales[:, g, v0:v1], grouped[:].rearrange("p v t -> p (v t)"))

        def multiply(v0, v1):
            bank = ps_h.tile([P, V], F32, name="h_bank")
            for g in range(PASSES):
                nc.tensor.matmul_mx(
                    out=bank[:, : v1 - v0],
                    lhsT=w2_codes[:, g, :].bitcast(FP8X4),
                    lhsT_scale=w2_scales[:, g, :],
                    rhs=z_codes[:, g, v0:v1].bitcast(FP8X4),
                    rhs_scale=z_scales[:, g, v0:v1],
                    start=(g == 0),
                    stop=(g == PASSES - 1),
                )
            return bank

        def store(v0, v1, bank, on_vector):
            result = keep.tile([P, v1 - v0], F32, name=f"result{v0}")
            if on_vector:
                nc.vector.tensor_copy(out=result[:], in_=bank[:, : v1 - v0])
            else:
                nc.scalar.copy(out=result[:], in_=bank[:, : v1 - v0])
            nc.sync.dma_start(out=out[:, v0:v1], in_=result[:])

        def prepare_w2():
            w2_grouped = keep.tile([P, PASSES, N, PACK], BF16, align_bytes=64, name="w2_grouped")
            nc.scalar.copy(out=w2_grouped[:], in_=w2_raw[:].rearrange("p g j c -> p g c j"))
            quantize(
                w2_codes[:].rearrange("p g c -> p (g c)"),
                w2_scales[:].rearrange("p g c -> p (g c)"),
                w2_grouped[:].rearrange("p g c j -> p (g c j)"),
            )

        prepare_w1(0, True)
        hs = [hpool.tile([P, T], F32, name="h")]
        for n, (g, a, b) in enumerate(x_loads):
            quantize_x(n, 0, b - a, copy_x(n, 0, b - a, "v"))
        project(0, ((0, 512, ((0, 512),)), (512, 1024, ((512, 768), (768, 1024)))), hs[0], last_on_vector=768)
        whole = ((0, 512, ((0, 512),)), (512, 1024, ((512, 1024),)))
        picked = []
        for b in range(BLOCKS - 1):
            hs.append(hpool.tile([P, T], F32, name="h"))
            now = []
            for d in range(D):
                now.append(gather(b, d, 0, V))
                if (b, d + 1) in behind:
                    prepare_w1(behind[b, d + 1], False)
                if (b, d) == (5, 2):
                    prepare_w2()
                if (b, d) == (5, 1):
                    z0 = turn_back(0, 0, V)
                if (b, d) == (6, 1):
                    quantize_z(0, 0, V, z0)
                if d == 0:
                    project(b + 1, whole, hs[b + 1])
                    if b > 0:
                        add_up(b - 1, picked, 0, V)
            picked = now
        b = BLOCKS - 1
        parts = ((0, 256), (256, 384), (384, 512))
        last = [[gather(b, d, *parts[0]) for d in range(D)]]
        add_up(b - 1, picked, 0, V)
        for part in parts[1:]:
            last.append([gather(b, d, *part) for d in range(D)])
        add_up(b, last[0], *parts[0])
        zA = turn_back(1, *parts[0])
        add_up(b, last[1], *parts[1])
        quantize_z(1, *parts[0], zA)
        add_up(b, last[2], *parts[2])
        zB = turn_back(1, *parts[1])
        quantize_z(1, *parts[1], zB)
        bank0 = multiply(*parts[0])
        zC = turn_back(1, *parts[2])
        quantize_z(1, *parts[2], zC)
        bank1 = multiply(*parts[1])
        bank2 = multiply(*parts[2])
        store(*parts[0], bank0, True)
        store(*parts[1], bank1, True)
        store(*parts[2], bank2, False)
